import numpy as np
import ml_dtypes


def mxq(x, axis, fmt="e4m3"):
    dtype, down = {"e4m3": (ml_dtypes.float8_e4m3fn, 7), "e5m2": (ml_dtypes.float8_e5m2, 14)}[fmt]
    v = np.moveaxis(np.asarray(x, np.float32).astype(ml_dtypes.bfloat16).astype(np.float64), axis, -1)
    blocks = v.reshape(v.shape[:-1] + (-1, 32))
    amax = np.abs(blocks).max(-1, keepdims=True)
    byte = np.maximum(np.where(amax > 0, np.frexp(amax)[1] - 1 + 127, 0) - down, 1)
    scale = np.exp2(byte - 127.0)
    codes = (blocks / scale).astype(np.float32).astype(dtype).astype(np.float64)
    return np.moveaxis((codes * scale).reshape(v.shape), -1, axis)


WIDE = False


def mx_kscale(k, group=512):
    if not WIDE:
        return np.ones(k)
    levels = np.array([10, -10, 5, -5, 0])
    if group != 512:
        return np.exp2(np.random.permutation(np.resize(levels, k // group))).repeat(group)
    if k % 512:
        return np.exp2(np.random.permutation(np.resize(levels, k // 32))).repeat(32)
    a = np.empty((k // 512, 16))
    for p in range(k // 512):
        a[p, :8] = np.random.permutation(np.resize(levels, 8))
        for g in range(8):
            far = levels[np.abs(levels - a[p, g]) >= 10]
            a[p, g + 8] = far[np.random.randint(len(far))]
    return np.exp2(a.ravel()).repeat(32)


def f64(x):
    return np.asarray(x).astype(np.float64)


E2M1 = np.array([0.0, 0.5, 1.0, 1.5, 2.0, 3.0, 4.0, 6.0, -0.0, -0.5, -1.0, -1.5, -2.0, -3.0, -4.0, -6.0])


def pack_group(w):
    k, n = w.shape
    w = f64(np.asarray(w, np.float32).astype(ml_dtypes.bfloat16)).reshape(k // 32, 32, n)
    amax = np.abs(w).max(1)
    mant, ex = np.frexp(amax / 6.0)
    byte = np.clip(np.where(amax > 0, np.where(mant > 0.5, ex, ex - 1) + 127, 1), 1, 254)
    scaled = (w * np.exp2(127.0 - byte)[:, None, :]).reshape(k, n).astype(np.float32)
    c = np.ascontiguousarray(scaled.reshape(k // 4, 4, n).transpose(0, 2, 1)).astype(ml_dtypes.float4_e2m1fn).view(np.uint8) & 0xF
    return np.ascontiguousarray((c[..., 0::2] | (c[..., 1::2] << 4)).reshape(k // 4, 2 * n)), byte.astype(np.uint8)


def unpack_group(words, scales):
    p, n = words.shape[0], scales.shape[1]
    words = np.ascontiguousarray(words).reshape(p, n, 2)
    nib = np.empty((p, n, 4), np.uint8)
    nib[..., 0::2] = words & 0xF
    nib[..., 1::2] = words >> 4
    return E2M1[nib].transpose(0, 2, 1).reshape(4 * p, n) * np.repeat(np.exp2(scales.astype(np.float64) - 127.0), 32, axis=0)


G, D, M, N = 2, 256, 256, 512


def setup_inputs():
    n = np.random.standard_normal
    s = mx_kscale(D, 0)[:, None]
    w_ = [pack_group(w) for w in n((G, D, M)) / np.sqrt(D) / s]
    u_ = [pack_group(w) for w in n((G, D, M)) / np.sqrt(D) / s]
    return {
        "x": (n((G, D, N)) * s).astype(np.float32),
        "w_words": np.stack([w[0] for w in w_]),
        "w_scales": np.stack([w[1] for w in w_]),
        "u_words": np.stack([w[0] for w in u_]),
        "u_scales": np.stack([w[1] for w in u_]),
        "b": (0.5 * n((G, M, 1))).astype(np.float32),
        "r": n((G, M, N)).astype(np.float32),
    }


def reference(x, w_words, w_scales, u_words, u_scales, b, r):
    xq = mxq(f64(x), 1, "e4m3")
    h = np.stack([unpack_group(w_words[g], w_scales[g]) for g in range(G)]).transpose(0, 2, 1) @ xq
    g = np.stack([unpack_group(u_words[g], u_scales[g]) for g in range(G)]).transpose(0, 2, 1) @ xq
    h = h + f64(b)
    y = np.maximum(h, 0.0) * g
    y = y + f64(r)
    return y

@@ -1,0 +1,132 @@
+from contextlib import ExitStack
+
+import concourse.mybir as mybir
+
+G, D, M, N = 2, 256, 256, 512
+FLOPS = 2 * 2 * G * D * M * N
+
+F32 = mybir.dt.float32
+BF16 = mybir.dt.bfloat16
+I32 = mybir.dt.int32
+U32 = mybir.dt.uint32
+U8 = mybir.dt.uint8
+FP8X4 = mybir.dt.float8_e4m3fn_x4
+FP4X4 = mybir.dt.float4_e2m1fn_x4
+RELU = mybir.ActivationFunctionType.Relu
+MULT = mybir.AluOpType.mult
+ADD = mybir.AluOpType.add
+
+P = 128
+PACK = 4
+ROWS = D // PACK
+QUAD = 32
+SCALE_ROWS = 4
+M_TILES = M // P
+HALF = N // 2
+VECTOR_COLS = 344
+
+
+def tile_rows_gglu_relu_bias_res_kernel(tc, x, w_words, w_scales, u_words, u_scales, b, r, out):
+    nc = tc.nc
+    tiles = [(g, t) for t in range(M_TILES) for g in range(G)]
+
+    with ExitStack() as ctx:
+        sb = ctx.enter_context(tc.tile_pool(name="sb", bufs=1))
+        psum = ctx.enter_context(tc.psum_pool(name="psum", bufs=1))
+        ctx.enter_context(tc.manual_schedule())
+
+        x_raw = sb.tile([P, PACK, N], F32, align_bytes=64)
+        x_bf = sb.tile([P, N, PACK], BF16, align_bytes=64)
+        x_codes = sb.tile([P, N], U32, align_bytes=64)
+        x_scale = sb.tile([P, N], U8, align_bytes=64)
+        w_sb = sb.tile([P, 2 * M], U8, align_bytes=64)
+        u_sb = sb.tile([P, 2 * M], U8, align_bytes=64)
+        wu_scale = sb.tile([P, 2 * M], U8, align_bytes=64)
+        b_rows = sb.tile([P, P], F32, align_bytes=64)
+        b_cols = sb.tile([P, P], F32, align_bytes=64)
+        w_scale = wu_scale[:, 0:M]
+        u_scale = wu_scale[:, M : 2 * M]
+
+        nc.vector.memset(wu_scale[:].bitcast(I32), 0)
+        nc.vector.memset(b_rows[:], 0.0)
+
+        def load_scales(plane, scales, g):
+            rows = scales.rearrange("g f m -> (g f) m")
+            for q in range(2 * g, 2 * g + 2):
+                nc.sync.dma_start(
+                    out=plane[QUAD * q : QUAD * q + SCALE_ROWS, :].bitcast(I32),
+                    in_=rows[SCALE_ROWS * q : SCALE_ROWS * (q + 1), :].bitcast(I32),
+                )
+
+        nc.sync.dma_start(out=x_raw[:], in_=x.rearrange("g (p j) n -> (g p) j n", j=PACK))
+        nc.sync.dma_start(out=w_sb[:].bitcast(I32), in_=w_words.rearrange("g p c -> (g p) c").bitcast(I32))
+        nc.sync.dma_start(out=u_sb[:].bitcast(I32), in_=u_words.rearrange("g p c -> (g p) c").bitcast(I32))
+        load_scales(w_scale, w_scales, 0)
+        load_scales(u_scale, u_scales, 0)
+        nc.sync.dma_start(
+            out=b_rows[0:P:QUAD, :].rearrange("a (c i) -> a c i", i=QUAD),
+            in_=b.rearrange("g (t a i) o -> a (g t) (i o)", t=M_TILES, i=QUAD),
+        )
+        load_scales(w_scale, w_scales, 1)
+        load_scales(u_scale, u_scales, 1)
+        r_sb = []
+        for g, t in tiles:
+            r_tile = sb.tile([P, N], F32, name=f"r_{g}_{t}")
+            nc.sync.dma_start(out=r_tile[:], in_=r[g, P * t : P * (t + 1), :])
+            r_sb.append(r_tile)
+
+        def views(lo, hi):
+            dst = x_bf[:, lo:hi, :].rearrange("p (c i) j -> p c j i", i=4)
+            src = x_raw[:, :, lo:hi].rearrange("p j (c i) -> p c j i", i=4)
+            return dst, src
+
+        def quantize(lo, hi):
+            nc.vector.quantize_mx(
+                out=x_codes[:, lo:hi].bitcast(FP8X4),
+                scales=x_scale[:, lo:hi],
+                in_=x_bf[:, lo:hi, :].rearrange("p n j -> p (n j)"),
+            )
+
+        for lo, hi in ((0, HALF), (HALF, VECTOR_COLS)):
+            dst, src = views(lo, hi)
+            nc.vector.tensor_copy(out=dst, in_=src)
+        dst, src = views(VECTOR_COLS, N)
+        nc.scalar.copy(out=dst, in_=src)
+        quantize(0, HALF)
+        quantize(HALF, N)
+        nc.vector.transpose(out=b_cols[:], in_=b_rows[:])
+
+        def product(name, words, plane, g, t):
+            rows = slice(ROWS * g, ROWS * (g + 1))
+            acc = psum.tile([P, N], F32, name=name)
+            nc.tensor.matmul_mx(
+                out=acc[:],
+                lhsT=words[rows, 2 * P * t : 2 * P * (t + 1)].bitcast(FP4X4),
+                lhsT_scale=plane[rows, P * t : P * (t + 1)],
+                rhs=x_codes[rows, :].bitcast(FP8X4),
+                rhs_scale=x_scale[rows, :],
+                start=True,
+                stop=True,
+            )
+            return acc
+
+        gated = []
+
+        def finish(i):
+            g, t = tiles[i]
+            y = sb.tile([P, N], F32, name=f"y_{g}_{t}")
+            nc.vector.tensor_tensor(out=y[:], in0=gated[i][:], in1=r_sb[i][:], op=ADD)
+            nc.sync.dma_start(out=out[g, P * t : P * (t + 1), :], in_=y[:])
+
+        for i, (g, t) in enumerate(tiles):
+            z = product(f"z_{g}_{t}", w_sb, w_scale, g, t)
+            lin = product(f"lin_{g}_{t}", u_sb, u_scale, g, t)
+            act = sb.tile([P, N], F32, name=f"act_{g}_{t}")
+            c = QUAD * (M_TILES * g + t)
+            nc.scalar.activation(out=act[:], in_=z[:], func=RELU, bias=b_cols[:, c : c + 1])
+            prod = sb.tile([P, N], F32, name=f"prod_{g}_{t}")
+            nc.vector.tensor_tensor(out=prod[:], in0=lin[:], in1=act[:], op=MULT)
+            gated.append(prod)
+            if i > 0:
+                finish(i - 1)
+        finish(len(tiles) - 1)

@@ -112,11 +112,11 @@ def tile_rows_gglu_relu_bias_res_kernel(tc, x, w_words, w_scales, u_words, u_sca
 
         gated = []
 
-        def finish(i):
+        def finish(engine, i, lo, hi):
             g, t = tiles[i]
-            y = sb.tile([P, N], F32, name=f"y_{g}_{t}")
-            nc.vector.tensor_tensor(out=y[:], in0=gated[i][:], in1=r_sb[i][:], op=ADD)
-            nc.sync.dma_start(out=out[g, P * t : P * (t + 1), :], in_=y[:])
+            y = sb.tile([P, hi - lo], F32, name=f"y_{g}_{t}_{lo}")
+            engine.tensor_tensor(out=y[:], in0=gated[i][:, lo:hi], in1=r_sb[i][:, lo:hi], op=ADD)
+            nc.sync.dma_start(out=out[g, P * t : P * (t + 1), lo:hi], in_=y[:])
 
         for i, (g, t) in enumerate(tiles):
             z = product(f"z_{g}_{t}", w_sb, w_scale, g, t)
@@ -127,6 +127,8 @@ def tile_rows_gglu_relu_bias_res_kernel(tc, x, w_words, w_scales, u_words, u_sca
             prod = sb.tile([P, N], F32, name=f"prod_{g}_{t}")
             nc.vector.tensor_tensor(out=prod[:], in0=lin[:], in1=act[:], op=MULT)
             gated.append(prod)
-            if i > 0:
-                finish(i - 1)
-        finish(len(tiles) - 1)
+        finish(nc.gpsimd, 0, 0, N)
+        finish(nc.vector, 1, 0, N)
+        finish(nc.vector, 2, 0, N)
+        finish(nc.vector, 3, 0, HALF)
+        finish(nc.vector, 3, HALF, N)

@@ -23,7 +23,8 @@ QUAD = 32
 SCALE_ROWS = 4
 M_TILES = M // P
 HALF = N // 2
-VECTOR_COLS = 344
+QUARTER = N // 4
+VECTOR_COLS = 304
 
 
 def tile_rows_gglu_relu_bias_res_kernel(tc, x, w_words, w_scales, u_words, u_scales, b, r, out):
@@ -50,10 +51,10 @@ def tile_rows_gglu_relu_bias_res_kernel(tc, x, w_words, w_scales, u_words, u_sca
         nc.vector.memset(wu_scale[:].bitcast(I32), 0)
         nc.vector.memset(b_rows[:], 0.0)
 
-        def load_scales(plane, scales, g):
+        def load_scales(queue, plane, scales, g):
             rows = scales.rearrange("g f m -> (g f) m")
             for q in range(2 * g, 2 * g + 2):
-                nc.sync.dma_start(
+                queue.dma_start(
                     out=plane[QUAD * q : QUAD * q + SCALE_ROWS, :].bitcast(I32),
                     in_=rows[SCALE_ROWS * q : SCALE_ROWS * (q + 1), :].bitcast(I32),
                 )
@@ -61,14 +62,14 @@ def tile_rows_gglu_relu_bias_res_kernel(tc, x, w_words, w_scales, u_words, u_sca
         nc.sync.dma_start(out=x_raw[:], in_=x.rearrange("g (p j) n -> (g p) j n", j=PACK))
         nc.sync.dma_start(out=w_sb[:].bitcast(I32), in_=w_words.rearrange("g p c -> (g p) c").bitcast(I32))
         nc.sync.dma_start(out=u_sb[:].bitcast(I32), in_=u_words.rearrange("g p c -> (g p) c").bitcast(I32))
-        load_scales(w_scale, w_scales, 0)
-        load_scales(u_scale, u_scales, 0)
+        load_scales(nc.sync, w_scale, w_scales, 0)
+        load_scales(nc.sync, u_scale, u_scales, 0)
         nc.sync.dma_start(
             out=b_rows[0:P:QUAD, :].rearrange("a (c i) -> a c i", i=QUAD),
             in_=b.rearrange("g (t a i) o -> a (g t) (i o)", t=M_TILES, i=QUAD),
         )
-        load_scales(w_scale, w_scales, 1)
-        load_scales(u_scale, u_scales, 1)
+        load_scales(nc.gpsimd, w_scale, w_scales, 1)
+        load_scales(nc.gpsimd, u_scale, u_scales, 1)
         r_sb = []
         for g, t in tiles:
             r_tile = sb.tile([P, N], F32, name=f"r_{g}_{t}")
@@ -87,13 +88,14 @@ def tile_rows_gglu_relu_bias_res_kernel(tc, x, w_words, w_scales, u_words, u_sca
                 in_=x_bf[:, lo:hi, :].rearrange("p n j -> p (n j)"),
             )
 
-        for lo, hi in ((0, HALF), (HALF, VECTOR_COLS)):
+        for lo, hi in ((0, QUARTER), (QUARTER, HALF), (HALF, VECTOR_COLS)):
             dst, src = views(lo, hi)
             nc.vector.tensor_copy(out=dst, in_=src)
-        dst, src = views(VECTOR_COLS, N)
-        nc.scalar.copy(out=dst, in_=src)
-        quantize(0, HALF)
-        quantize(HALF, N)
+        for lo, hi in ((VECTOR_COLS, 3 * QUARTER), (3 * QUARTER, N)):
+            dst, src = views(lo, hi)
+            nc.scalar.copy(out=dst, in_=src)
+        for lo in range(0, N, QUARTER):
+            quantize(lo, lo + QUARTER)
         nc.vector.transpose(out=b_cols[:], in_=b_rows[:])
 
         def product(name, words, plane, g, t):

@@ -68,8 +68,8 @@ def tile_rows_gglu_relu_bias_res_kernel(tc, x, w_words, w_scales, u_words, u_sca
             out=b_rows[0:P:QUAD, :].rearrange("a (c i) -> a c i", i=QUAD),
             in_=b.rearrange("g (t a i) o -> a (g t) (i o)", t=M_TILES, i=QUAD),
         )
-        load_scales(nc.gpsimd, w_scale, w_scales, 1)
-        load_scales(nc.gpsimd, u_scale, u_scales, 1)
+        load_scales(nc.sync, w_scale, w_scales, 1)
+        load_scales(nc.sync, u_scale, u_scales, 1)
         r_sb = []
         for g, t in tiles:
             r_tile = sb.tile([P, N], F32, name=f"r_{g}_{t}")
@@ -132,5 +132,4 @@ def tile_rows_gglu_relu_bias_res_kernel(tc, x, w_words, w_scales, u_words, u_sca
         finish(nc.gpsimd, 0, 0, N)
         finish(nc.vector, 1, 0, N)
         finish(nc.vector, 2, 0, N)
-        finish(nc.vector, 3, 0, HALF)
-        finish(nc.vector, 3, HALF, N)
+        finish(nc.vector, 3, 0, N)

@@ -24,7 +24,8 @@ SCALE_ROWS = 4
 M_TILES = M // P
 HALF = N // 2
 QUARTER = N // 4
-VECTOR_COLS = 304
+RUN = 4
+VECTOR_COLS = 160
 
 
 def tile_rows_gglu_relu_bias_res_kernel(tc, x, w_words, w_scales, u_words, u_scales, b, r, out):
@@ -36,7 +37,7 @@ def tile_rows_gglu_relu_bias_res_kernel(tc, x, w_words, w_scales, u_words, u_sca
         psum = ctx.enter_context(tc.psum_pool(name="psum", bufs=1))
         ctx.enter_context(tc.manual_schedule())
 
-        x_raw = sb.tile([P, PACK, N], F32, align_bytes=64)
+        x_raw = [sb.tile([P, PACK, HALF], F32, name=f"x_raw_{h}", align_bytes=64) for h in range(2)]
         x_bf = sb.tile([P, N, PACK], BF16, align_bytes=64)
         x_codes = sb.tile([P, N], U32, align_bytes=64)
         x_scale = sb.tile([P, N], U8, align_bytes=64)
@@ -51,60 +52,59 @@ def tile_rows_gglu_relu_bias_res_kernel(tc, x, w_words, w_scales, u_words, u_sca
         nc.vector.memset(wu_scale[:].bitcast(I32), 0)
         nc.vector.memset(b_rows[:], 0.0)
 
-        def load_scales(queue, plane, scales, g):
+        def load_scales(scale_sb, scales, g):
             rows = scales.rearrange("g f m -> (g f) m")
             for q in range(2 * g, 2 * g + 2):
-                queue.dma_start(
-                    out=plane[QUAD * q : QUAD * q + SCALE_ROWS, :].bitcast(I32),
+                nc.sync.dma_start(
+                    out=scale_sb[QUAD * q : QUAD * q + SCALE_ROWS, :].bitcast(I32),
                     in_=rows[SCALE_ROWS * q : SCALE_ROWS * (q + 1), :].bitcast(I32),
                 )
 
-        nc.sync.dma_start(out=x_raw[:], in_=x.rearrange("g (p j) n -> (g p) j n", j=PACK))
-        nc.sync.dma_start(out=w_sb[:].bitcast(I32), in_=w_words.rearrange("g p c -> (g p) c").bitcast(I32))
-        nc.sync.dma_start(out=u_sb[:].bitcast(I32), in_=u_words.rearrange("g p c -> (g p) c").bitcast(I32))
-        load_scales(nc.sync, w_scale, w_scales, 0)
-        load_scales(nc.sync, u_scale, u_scales, 0)
+        x_rows = x.rearrange("g (p j) n -> (g p) j n", j=PACK)
+        nc.sync.dma_start(out=x_raw[0][:], in_=x_rows[:, :, 0:HALF])
+        load_scales(w_scale, w_scales, 0)
+        load_scales(u_scale, u_scales, 0)
         nc.sync.dma_start(
             out=b_rows[0:P:QUAD, :].rearrange("a (c i) -> a c i", i=QUAD),
             in_=b.rearrange("g (t a i) o -> a (g t) (i o)", t=M_TILES, i=QUAD),
         )
-        load_scales(nc.sync, w_scale, w_scales, 1)
-        load_scales(nc.sync, u_scale, u_scales, 1)
+        nc.sync.dma_start(out=x_raw[1][:], in_=x_rows[:, :, HALF:N])
+        nc.sync.dma_start(out=w_sb[:].bitcast(I32), in_=w_words.rearrange("g p c -> (g p) c").bitcast(I32))
+        nc.sync.dma_start(out=u_sb[:].bitcast(I32), in_=u_words.rearrange("g p c -> (g p) c").bitcast(I32))
+        load_scales(w_scale, w_scales, 1)
+        load_scales(u_scale, u_scales, 1)
         r_sb = []
         for g, t in tiles:
             r_tile = sb.tile([P, N], F32, name=f"r_{g}_{t}")
             nc.sync.dma_start(out=r_tile[:], in_=r[g, P * t : P * (t + 1), :])
             r_sb.append(r_tile)
 
-        def views(lo, hi):
-            dst = x_bf[:, lo:hi, :].rearrange("p (c i) j -> p c j i", i=4)
-            src = x_raw[:, :, lo:hi].rearrange("p j (c i) -> p c j i", i=4)
+        def interleave_views(h, lo, hi):
+            dst = x_bf[:, HALF * h + lo : HALF * h + hi, :].rearrange("p (c i) j -> p c j i", i=RUN)
+            src = x_raw[h][:, :, lo:hi].rearrange("p j (c i) -> p c j i", i=RUN)
             return dst, src
 
-        def quantize(lo, hi):
-            nc.vector.quantize_mx(
-                out=x_codes[:, lo:hi].bitcast(FP8X4),
-                scales=x_scale[:, lo:hi],
-                in_=x_bf[:, lo:hi, :].rearrange("p n j -> p (n j)"),
-            )
-
-        for lo, hi in ((0, QUARTER), (QUARTER, HALF), (HALF, VECTOR_COLS)):
-            dst, src = views(lo, hi)
-            nc.vector.tensor_copy(out=dst, in_=src)
-        for lo, hi in ((VECTOR_COLS, 3 * QUARTER), (3 * QUARTER, N)):
-            dst, src = views(lo, hi)
+        for h in range(2):
+            for lo, hi in ((0, QUARTER), (QUARTER, VECTOR_COLS)):
+                dst, src = interleave_views(h, lo, hi)
+                nc.vector.tensor_copy(out=dst, in_=src)
+            dst, src = interleave_views(h, VECTOR_COLS, HALF)
             nc.scalar.copy(out=dst, in_=src)
-        for lo in range(0, N, QUARTER):
-            quantize(lo, lo + QUARTER)
+            for lo in range(HALF * h, HALF * (h + 1), QUARTER):
+                nc.vector.quantize_mx(
+                    out=x_codes[:, lo : lo + QUARTER].bitcast(FP8X4),
+                    scales=x_scale[:, lo : lo + QUARTER],
+                    in_=x_bf[:, lo : lo + QUARTER, :].rearrange("p n j -> p (n j)"),
+                )
         nc.vector.transpose(out=b_cols[:], in_=b_rows[:])
 
-        def product(name, words, plane, g, t):
+        def product(name, words, scale_sb, g, t):
             rows = slice(ROWS * g, ROWS * (g + 1))
             acc = psum.tile([P, N], F32, name=name)
             nc.tensor.matmul_mx(
                 out=acc[:],
                 lhsT=words[rows, 2 * P * t : 2 * P * (t + 1)].bitcast(FP4X4),
-                lhsT_scale=plane[rows, P * t : P * (t + 1)],
+                lhsT_scale=scale_sb[rows, P * t : P * (t + 1)],
                 rhs=x_codes[rows, :].bitcast(FP8X4),
                 rhs_scale=x_scale[rows, :],
                 start=True,
@@ -113,23 +113,18 @@ def tile_rows_gglu_relu_bias_res_kernel(tc, x, w_words, w_scales, u_words, u_sca
             return acc
 
         gated = []
-
-        def finish(engine, i, lo, hi):
-            g, t = tiles[i]
-            y = sb.tile([P, hi - lo], F32, name=f"y_{g}_{t}_{lo}")
-            engine.tensor_tensor(out=y[:], in0=gated[i][:, lo:hi], in1=r_sb[i][:, lo:hi], op=ADD)
-            nc.sync.dma_start(out=out[g, P * t : P * (t + 1), lo:hi], in_=y[:])
-
-        for i, (g, t) in enumerate(tiles):
+        for g, t in tiles:
             z = product(f"z_{g}_{t}", w_sb, w_scale, g, t)
             lin = product(f"lin_{g}_{t}", u_sb, u_scale, g, t)
             act = sb.tile([P, N], F32, name=f"act_{g}_{t}")
-            c = QUAD * (M_TILES * g + t)
-            nc.scalar.activation(out=act[:], in_=z[:], func=RELU, bias=b_cols[:, c : c + 1])
+            bias_col = QUAD * (M_TILES * g + t)
+            nc.scalar.activation(out=act[:], in_=z[:], func=RELU, bias=b_cols[:, bias_col : bias_col + 1])
             prod = sb.tile([P, N], F32, name=f"prod_{g}_{t}")
             nc.vector.tensor_tensor(out=prod[:], in0=lin[:], in1=act[:], op=MULT)
             gated.append(prod)
-        finish(nc.gpsimd, 0, 0, N)
-        finish(nc.vector, 1, 0, N)
-        finish(nc.vector, 2, 0, N)
-        finish(nc.vector, 3, 0, N)
+
+        for i, (g, t) in enumerate(tiles):
+            engine = nc.gpsimd if i == 0 else nc.vector
+            y = sb.tile([P, N], F32, name=f"y_{g}_{t}")
+            engine.tensor_tensor(out=y[:], in0=gated[i][:], in1=r_sb[i][:], op=ADD)
+            nc.sync.dma_start(out=out[g, P * t : P * (t + 1), :], in_=y[:])

from contextlib import ExitStack

import concourse.mybir as mybir

G, D, M, N = 2, 256, 256, 512
FLOPS = 2 * 2 * G * D * M * N

F32 = mybir.dt.float32
BF16 = mybir.dt.bfloat16
I32 = mybir.dt.int32
U32 = mybir.dt.uint32
U8 = mybir.dt.uint8
FP8X4 = mybir.dt.float8_e4m3fn_x4
FP4X4 = mybir.dt.float4_e2m1fn_x4
RELU = mybir.ActivationFunctionType.Relu
MULT = mybir.AluOpType.mult
ADD = mybir.AluOpType.add

P = 128
PACK = 4
ROWS = D // PACK
QUAD = 32
SCALE_ROWS = 4
M_TILES = M // P
HALF = N // 2
QUARTER = N // 4
RUN = 4
VECTOR_COLS = 160


def tile_rows_gglu_relu_bias_res_kernel(tc, x, w_words, w_scales, u_words, u_scales, b, r, out):
    nc = tc.nc
    tiles = [(g, t) for t in range(M_TILES) for g in range(G)]

    with ExitStack() as ctx:
        sb = ctx.enter_context(tc.tile_pool(name="sb", bufs=1))
        psum = ctx.enter_context(tc.psum_pool(name="psum", bufs=1))
        ctx.enter_context(tc.manual_schedule())

        x_raw = [sb.tile([P, PACK, HALF], F32, name=f"x_raw_{h}", align_bytes=64) for h in range(2)]
        x_bf = sb.tile([P, N, PACK], BF16, align_bytes=64)
        x_codes = sb.tile([P, N], U32, align_bytes=64)
        x_scale = sb.tile([P, N], U8, align_bytes=64)
        w_sb = sb.tile([P, 2 * M], U8, align_bytes=64)
        u_sb = sb.tile([P, 2 * M], U8, align_bytes=64)
        wu_scale = sb.tile([P, 2 * M], U8, align_bytes=64)
        b_rows = sb.tile([P, P], F32, align_bytes=64)
        b_cols = sb.tile([P, P], F32, align_bytes=64)
        w_scale = wu_scale[:, 0:M]
        u_scale = wu_scale[:, M : 2 * M]

        nc.vector.memset(wu_scale[:].bitcast(I32), 0)
        nc.vector.memset(b_rows[:], 0.0)

        def load_scales(scale_sb, scales, g):
            rows = scales.rearrange("g f m -> (g f) m")
            for q in range(2 * g, 2 * g + 2):
                nc.sync.dma_start(
                    out=scale_sb[QUAD * q : QUAD * q + SCALE_ROWS, :].bitcast(I32),
                    in_=rows[SCALE_ROWS * q : SCALE_ROWS * (q + 1), :].bitcast(I32),
                )

        x_rows = x.rearrange("g (p j) n -> (g p) j n", j=PACK)
        nc.sync.dma_start(out=x_raw[0][:], in_=x_rows[:, :, 0:HALF])
        load_scales(w_scale, w_scales, 0)
        load_scales(u_scale, u_scales, 0)
        nc.sync.dma_start(
            out=b_rows[0:P:QUAD, :].rearrange("a (c i) -> a c i", i=QUAD),
            in_=b.rearrange("g (t a i) o -> a (g t) (i o)", t=M_TILES, i=QUAD),
        )
        nc.sync.dma_start(out=x_raw[1][:], in_=x_rows[:, :, HALF:N])
        nc.sync.dma_start(out=w_sb[:].bitcast(I32), in_=w_words.rearrange("g p c -> (g p) c").bitcast(I32))
        nc.sync.dma_start(out=u_sb[:].bitcast(I32), in_=u_words.rearrange("g p c -> (g p) c").bitcast(I32))
        load_scales(w_scale, w_scales, 1)
        load_scales(u_scale, u_scales, 1)
        r_sb = []
        for g, t in tiles:
            r_tile = sb.tile([P, N], F32, name=f"r_{g}_{t}")
            nc.sync.dma_start(out=r_tile[:], in_=r[g, P * t : P * (t + 1), :])
            r_sb.append(r_tile)

        def interleave_views(h, lo, hi):
            dst = x_bf[:, HALF * h + lo : HALF * h + hi, :].rearrange("p (c i) j -> p c j i", i=RUN)
            src = x_raw[h][:, :, lo:hi].rearrange("p j (c i) -> p c j i", i=RUN)
            return dst, src

        for h in range(2):
            for lo, hi in ((0, QUARTER), (QUARTER, VECTOR_COLS)):
                dst, src = interleave_views(h, lo, hi)
                nc.vector.tensor_copy(out=dst, in_=src)
            dst, src = interleave_views(h, VECTOR_COLS, HALF)
            nc.scalar.copy(out=dst, in_=src)
            for lo in range(HALF * h, HALF * (h + 1), QUARTER):
                nc.vector.quantize_mx(
                    out=x_codes[:, lo : lo + QUARTER].bitcast(FP8X4),
                    scales=x_scale[:, lo : lo + QUARTER],
                    in_=x_bf[:, lo : lo + QUARTER, :].rearrange("p n j -> p (n j)"),
                )
        nc.vector.transpose(out=b_cols[:], in_=b_rows[:])

        def product(name, words, scale_sb, g, t):
            rows = slice(ROWS * g, ROWS * (g + 1))
            acc = psum.tile([P, N], F32, name=name)
            nc.tensor.matmul_mx(
                out=acc[:],
                lhsT=words[rows, 2 * P * t : 2 * P * (t + 1)].bitcast(FP4X4),
                lhsT_scale=scale_sb[rows, P * t : P * (t + 1)],
                rhs=x_codes[rows, :].bitcast(FP8X4),
                rhs_scale=x_scale[rows, :],
                start=True,
                stop=True,
            )
            return acc

        gated = []
        for g, t in tiles:
            z = product(f"z_{g}_{t}", w_sb, w_scale, g, t)
            lin = product(f"lin_{g}_{t}", u_sb, u_scale, g, t)
            act = sb.tile([P, N], F32, name=f"act_{g}_{t}")
            bias_col = QUAD * (M_TILES * g + t)
            nc.scalar.activation(out=act[:], in_=z[:], func=RELU, bias=b_cols[:, bias_col : bias_col + 1])
            prod = sb.tile([P, N], F32, name=f"prod_{g}_{t}")
            nc.vector.tensor_tensor(out=prod[:], in0=lin[:], in1=act[:], op=MULT)
            gated.append(prod)

        for i, (g, t) in enumerate(tiles):
            engine = nc.gpsimd if i == 0 else nc.vector
            y = sb.tile([P, N], F32, name=f"y_{g}_{t}")
            engine.tensor_tensor(out=y[:], in0=gated[i][:], in1=r_sb[i][:], op=ADD)
            nc.sync.dma_start(out=out[g, P * t : P * (t + 1), :], in_=y[:])
